import numpy as np
import ml_dtypes


def mxq(x, axis, fmt="e4m3"):
    dtype, down = {"e4m3": (ml_dtypes.float8_e4m3fn, 7), "e5m2": (ml_dtypes.float8_e5m2, 14)}[fmt]
    v = np.moveaxis(np.asarray(x, np.float32).astype(ml_dtypes.bfloat16).astype(np.float64), axis, -1)
    blocks = v.reshape(v.shape[:-1] + (-1, 32))
    amax = np.abs(blocks).max(-1, keepdims=True)
    byte = np.maximum(np.where(amax > 0, np.frexp(amax)[1] - 1 + 127, 0) - down, 1)
    scale = np.exp2(byte - 127.0)
    codes = (blocks / scale).astype(np.float32).astype(dtype).astype(np.float64)
    return np.moveaxis((codes * scale).reshape(v.shape), -1, axis)


WIDE = False


def mx_kscale(k):
    if not WIDE:
        return np.ones(k)
    levels = np.array([10, -10, 5, -5, 0])
    if k % 512:
        return np.exp2(np.random.permutation(np.resize(levels, k // 32))).repeat(32)
    a = np.empty((k // 512, 16))
    for p in range(k // 512):
        a[p, :8] = np.random.permutation(np.resize(levels, 8))
        for g in range(8):
            far = levels[np.abs(levels - a[p, g]) >= 10]
            a[p, g + 8] = far[np.random.randint(len(far))]
    return np.exp2(a.ravel()).repeat(32)


def f64(x):
    return np.asarray(x).astype(np.float64)


def striped(idx):
    return np.tile(idx.reshape(-1, 16).T, (8, 1)).astype(np.uint16)


def unstriped(offs):
    return offs[:16].T.reshape(-1).astype(np.int64)


def striped8(idx):
    return np.concatenate([x.reshape(-1, 16).T for x in idx]).astype(np.uint16)


def runs(offs, k):
    lists = np.stack([offs[16 * r : 16 * r + 16].T.reshape(-1) for r in range(8)]).astype(np.int64)
    return lists[np.arange(k) % 512 // 64]


def pack_weight(w):
    k, n = w.shape
    w = f64(np.asarray(w, np.float32).astype(ml_dtypes.bfloat16)).reshape(k // 32, 32, n)
    amax = np.abs(w).max(1)
    byte = np.clip(np.where(amax > 0, np.frexp(amax)[1] - 1 + 127 - 7, 1), 1, 254)
    scaled = (w * np.exp2(127.0 - byte)[:, None, :]).reshape(k, n).astype(np.float32)
    words = np.ascontiguousarray(scaled.reshape(k // 512, 128, 4, n).transpose(0, 1, 3, 2)).astype(ml_dtypes.float8_e4m3fn).view(np.uint8)
    return words, np.ascontiguousarray(byte.astype(np.uint8).reshape(k // 512, 16, n))


def unpack_weight(words, scales):
    g, p, n, _ = words.shape
    vals = np.ascontiguousarray(words).view(ml_dtypes.float8_e4m3fn).astype(np.float64) * np.repeat(np.exp2(scales.astype(np.float64) - 127.0), 8, axis=1)[..., None]
    return vals.transpose(0, 1, 3, 2).reshape(g * 512, n)

def planes(y):
    n, m = y.shape
    v = y.astype(np.float32).astype(ml_dtypes.bfloat16).astype(np.float64).reshape(n // 32, 32, m)
    top = np.abs(v).max(1)
    byte = np.clip(np.where(top > 0, np.frexp(top)[1] - 1 + 127 - 7, 1), 1, 254)
    codes = (v * np.exp2(127.0 - byte)[:, None, :]).reshape(n, m).astype(np.float32).astype(ml_dtypes.float8_e4m3fn).view(np.uint8)
    words = codes.reshape(n // 512, 128, 4, m).transpose(0, 1, 3, 2)
    return np.ascontiguousarray(words), np.ascontiguousarray(byte.astype(np.uint8).reshape(n // 512, 16, m))


K, T, S, N, H = 512, 2048, 512, 512, 512


def setup_inputs():
    n = np.random.standard_normal
    s = mx_kscale(K)[:, None]
    u = mx_kscale(S)
    packed_xT = pack_weight(n((K, T)) * s)
    return {
        "x_words": packed_xT[0],
        "x_scales": packed_xT[1],
        "wa": (n((K, H)) / np.sqrt(K) / s).astype(np.float32),
        "wb": (n((K, N)) / np.sqrt(K) / s).astype(np.float32),
        "gt": (np.random.uniform(0.5, 1.5, (S, 1)) * u[:, None]).astype(np.float32),
        "gi": (np.random.uniform(0.5, 1.5, (S, 1)) / u[:, None]).astype(np.float32),
        "offs": striped(np.random.permutation(T)[:S]),
        "two": striped(np.random.permutation(T)[:S]),
        "fl": striped8(np.stack([np.random.permutation(N) for _ in range(8)])),
    }


def reference(x_words, x_scales, wa, wb, gt, gi, offs, two, fl):
    xq = unpack_weight(x_words, x_scales)[:, unstriped(offs)]
    a = xq.T @ mxq(f64(wa), 0, "e4m3")
    z = f64(gt) * a
    zq = mxq(z, 0, "e4m3")
    x_two = unpack_weight(x_words, x_scales)[:, unstriped(two)]
    b = x_two.T @ mxq(f64(wb), 0, "e4m3")
    z2 = f64(gi) * b
    d = b[np.arange(S)[:, None], runs(fl, S)]
    z3 = f64(gi) * d
    m1 = 0.03125 * ((zq.T @ mxq(z2, 0, "e4m3")) - ((zq.T @ mxq(z3, 0, "e4m3"))))
    out_0 = (m1) ** 2
    return (out_0,) + planes(out_0)

@@ -1,0 +1,227 @@
+from contextlib import ExitStack
+
+import concourse.mybir as mybir
+
+K, T, S, N, H = 512, 2048, 512, 512, 512
+FLOPS = 4 * 2 * 512 * 512 * 512
+
+F32 = mybir.dt.float32
+BF16 = mybir.dt.bfloat16
+I32 = mybir.dt.int32
+U32 = mybir.dt.uint32
+U16 = mybir.dt.uint16
+U8 = mybir.dt.uint8
+X4 = mybir.dt.float8_e4m3fn_x4
+ACT = mybir.ActivationFunctionType
+ALU = mybir.AluOpType
+P = 128
+HALF = 256
+
+
+def weave_views(dst, src):
+    return dst.rearrange("p (c i t) -> p c t i", i=4, t=4), src.rearrange("p t (c i) -> p c t i", i=4)
+
+
+def weave_v(nc, dst, src, scale=None):
+    d, s = weave_views(dst, src)
+    if scale is None:
+        nc.vector.tensor_copy(out=d, in_=s)
+    else:
+        nc.vector.tensor_scalar(out=d, in0=s, scalar1=scale, scalar2=None, op0=ALU.mult)
+
+
+def weave_s(nc, dst, src, scale=1.0):
+    d, s = weave_views(dst, src)
+    nc.scalar.activation(out=d, in_=s, func=ACT.Copy, scale=scale)
+
+
+def tile_picked_momdiff_square_po_kernel(tc, x_words, x_scales, wa, wb, gt, gi, offs, two, fl, out_0, out_1, out_2):
+    nc = tc.nc
+    with ExitStack() as ctx:
+        keep = ctx.enter_context(tc.tile_pool(name="keep", bufs=1))
+        psum = ctx.enter_context(tc.psum_pool(name="psum", bufs=1))
+
+        def tile(name, shape, dtype, tag=None):
+            return keep.tile(shape, dtype, name=name, tag=tag or name, align_bytes=64)
+
+        def quant(name, src, codes, scales):
+            nc.vector.quantize_mx(out=codes.bitcast(X4), scales=scales, in_=src)
+
+        two_t = keep.tile([P, 32], U16, name="two_t")
+        offs_t = keep.tile([P, 32], U16, name="offs_t")
+        fl_t = keep.tile([P, 32], U16, name="fl_t")
+        xw = tile("xw", [P, T], I32)
+        xs = tile("xs", [P, T], U8)
+        nc.vector.memset(xs[:].bitcast(I32), 0)
+        nc.sync.dma_start(two_t[:], two)
+        nc.sync.dma_start(offs_t[:], offs)
+        nc.sync.dma_start(fl_t[:], fl)
+        for q in range(4):
+            nc.sync.dma_start(out=xs[32 * q : 32 * q + 4, :].bitcast(I32), in_=x_scales[0, 4 * q : 4 * q + 4, :].bitcast(I32))
+        raw = {}
+        nc.sync.dma_start(out=xw[:], in_=x_words[0].rearrange("p n t -> p (n t)").bitcast(I32))
+        for nm, w in (("b", wb), ("a", wa)):
+            for h in range(2):
+                raw[nm, h] = tile("w%s_raw%d" % (nm, h), [P, 4, HALF], F32)
+                nc.sync.dma_start(out=raw[nm, h][:], in_=w.rearrange("(p j) n -> p j n", j=4)[:, :, h * HALF : (h + 1) * HALF])
+        gt_t = tile("gt_t", [P, 4], F32)
+        gi_t = tile("gi_t", [P, 4], F32)
+        nc.sync.dma_start(out=gi_t[:], in_=gi.rearrange("(p t) o -> p (t o)", t=4))
+        nc.sync.dma_start(out=gt_t[:], in_=gt.rearrange("(p t) o -> p (t o)", t=4))
+        warm = tile("warm", [P, 8], F32)
+        warm2 = tile("warm2", [P, 8], F32)
+        nc.gpsimd.memset(warm[:], 0.0)
+        nc.scalar.activation(out=warm2[:], in_=warm[:], func=ACT.Square)
+
+        def pick_scales(name, lst):
+            g = tile(name + "_g", [P, S], U8)
+            nc.vector.tensor_copy(out=g[:], in_=xs[:].indirect(lst[:]))
+            d = tile(name + "_d", [P, S], U8)
+            return g, d
+
+        def deal_scales(g, d):
+            nc.vector.tensor_copy(out=d[:].rearrange("p (t m) -> p t m", t=4), in_=g[:].rearrange("p (m t) -> p t m", t=4))
+
+        def pick_words(name, lst):
+            g = tile(name + "_w", [P, S], U32)
+            nc.vector.tensor_copy(out=g[:].rearrange("p (t m) -> p m t", t=4), in_=xw[:].bitcast(U32).indirect(lst[:]))
+            return g
+
+        def mm(out, lq, ls, rq, rs, start=True, stop=True):
+            nc.tensor.matmul_mx(out=out, lhsT=lq.bitcast(X4), lhsT_scale=ls, rhs=rq.bitcast(X4), rhs_scale=rs, start=start, stop=stop)
+
+        g2, s2 = pick_scales("two", two_t)
+        w2 = pick_words("two", two_t)
+        deal_scales(g2, s2)
+        g1, s1 = pick_scales("offs", offs_t)
+
+        wb_b = tile("wb_b", [P, 4 * N], BF16)
+        wb_q = tile("wb_q", [P, N], U32)
+        wb_s = tile("wb_s", [P, N], U8)
+        for h in range(2):
+            weave_s(nc, wb_b[:, 4 * HALF * h : 4 * HALF * (h + 1)], raw["b", h][:])
+        w1 = pick_words("offs", offs_t)
+        for h in range(2):
+            c = slice(h * HALF, (h + 1) * HALF)
+            quant("wb", wb_b[:, 4 * HALF * h : 4 * HALF * (h + 1)], wb_q[:, c], wb_s[:, c])
+        deal_scales(g1, s1)
+
+        banks = {}
+        for t in range(4):
+            banks["b", t] = psum.tile([P, N], F32, name="bank%d" % t)
+            c = slice(128 * t, 128 * (t + 1))
+            mm(banks["b", t][:], w2[:, c], s2[:, c], wb_q[:], wb_s[:])
+
+        wa_b = tile("wa_b", [P, 4 * H], BF16)
+        wa_q = tile("wa_q", [P, H], U32)
+        wa_s = tile("wa_s", [P, H], U8)
+        weave_s(nc, wa_b[:, 0 : 4 * HALF], raw["a", 0][:])
+        weave_v(nc, wa_b[:, 4 * HALF : 8 * HALF], raw["a", 1][:])
+        for h in range(2):
+            c = slice(h * HALF, (h + 1) * HALF)
+            quant("wa", wa_b[:, 4 * HALF * h : 4 * HALF * (h + 1)], wa_q[:, c], wa_s[:, c])
+
+        win = []
+        z2f = tile("z2f", [P, 4, N], F32)
+        for t in range(4):
+            wt = tile("win%d" % t, [P, N], F32)
+            win.append(wt)
+            nc.scalar.activation(out=wt[:], in_=banks["b", t][:], func=ACT.Copy, scale=gi_t[:, t : t + 1])
+            nc.sync.dma_start(out=z2f[:, t, :], in_=wt[:])
+
+        for t in range(4):
+            banks["a", t] = psum.tile([P, H], F32, name="bank%d" % (4 + t))
+            c = slice(128 * t, 128 * (t + 1))
+            mm(banks["a", t][:], w1[:, c], s1[:, c], wa_q[:], wa_s[:])
+
+        spans = [(0, 256), (256, 128), (384, 128)]
+        z3f = [tile("z3f%d" % i, [P, 4, w], F32) for i, (c0, w) in enumerate(spans[0:2])]
+        z3b = [tile("z3b%d" % i, [P, 4 * w], BF16) for i, (c0, w) in enumerate(spans)]
+        z3q = tile("z3q", [P, N], U32)
+        z3s = tile("z3s", [P, N], U8)
+        z2b = [tile("z2b%d" % h, [P, 4 * HALF], BF16) for h in range(2)]
+        z2q = tile("z2q", [P, N], U32)
+        z2s = tile("z2s", [P, N], U8)
+
+        def gather(i, ts):
+            c0, w = spans[i]
+            for t in ts:
+                nc.vector.tensor_copy(out=z3f[i][:, t, :], in_=win[t][:].indirect(fl_t[:, c0 // 16 : (c0 + w) // 16]))
+
+        def q3(i):
+            c0, w = spans[i]
+            quant("z3", z3b[i][:], z3q[:, c0 : c0 + w], z3s[:, c0 : c0 + w])
+
+        def q2(h):
+            quant("z2", z2b[h][:], z2q[:, h * HALF : (h + 1) * HALF], z2s[:, h * HALF : (h + 1) * HALF])
+
+        gather(0, range(4))
+        zp = tile("zp", [P, 4, H], BF16)
+        for t in range(4):
+            nc.scalar.activation(out=zp[:, t, :].rearrange("p (u m) -> p u m", u=4), in_=banks["a", t][:].rearrange("p (m u) -> p u m", u=4), func=ACT.Copy, scale=gt_t[:, t : t + 1])
+        gather(1, range(4))
+        z_b = [tile("z_b%d" % h, [P, 4 * HALF], BF16) for h in range(2)]
+        z_q = tile("z_q", [P, H], U32)
+        z_s = tile("z_s", [P, H], U8)
+        weave_s(nc, z_b[1][:], zp[:, :, HALF:H])
+        weave_v(nc, z3b[0][:], z3f[0][:], -1.0)
+        weave_v(nc, z_b[0][:], zp[:, :, 0:HALF])
+        q3(0)
+        weave_s(nc, z2b[0][:], z2f[:, :, 0:HALF])
+        for h in range(2):
+            quant("z", z_b[h][:], z_q[:, h * HALF : (h + 1) * HALF], z_s[:, h * HALF : (h + 1) * HALF])
+        weave_s(nc, z3b[1][:], z3f[1][:], -1.0)
+        q2(0)
+        weave_s(nc, z2b[1][:], z2f[:, :, HALF:N])
+        z3f.append(tile("z3f2", [P, 4, 128], F32, tag="z_b1"))
+
+        o_q = tile("o_q", [P, N], I32)
+        o_s = tile("o_s", [P, N], U8)
+        out_rows = out_0.rearrange("(p u) n -> p u n", u=4)
+        out_words = out_1[0].rearrange("p n t -> p (n t)").bitcast(I32)
+        y01 = tile("y01", [P, 4, HALF], F32)
+        ys = [y01[:, :, 0:128], y01[:, :, 128:256], tile("y2", [P, 4, 128], F32)[:], tile("y3", [P, 4, 128], F32)[:]]
+        y_b = tile("y_b", [P, 4 * N], BF16)
+        acc = {}
+
+        def product(ch):
+            acc[ch] = psum.tile([P, 4, 128], F32, name="bank%d" % ch)
+            cols = slice(128 * ch, 128 * (ch + 1))
+            for u in range(4):
+                c = slice(128 * u, 128 * (u + 1))
+                mm(acc[ch][:, u, :], z_q[:, c], z_s[:, c], z2q[:, cols], z2s[:, cols], True, False)
+                mm(acc[ch][:, u, :], z_q[:, c], z_s[:, c], z3q[:, cols], z3s[:, cols], False, True)
+
+        def square(ch):
+            nc.scalar.activation(out=ys[ch], in_=acc[ch][:], func=ACT.Square, scale=0.03125)
+
+        def qy(c0, w):
+            quant("y", y_b[:, 4 * c0 : 4 * (c0 + w)], o_q[:, c0 : c0 + w], o_s[:, c0 : c0 + w])
+
+        product(0)
+        product(1)
+        gather(2, range(4))
+        q3(1)
+        weave_v(nc, z3b[2][:], z3f[2][:], -1.0)
+        q2(1)
+        q3(2)
+        product(2)
+        product(3)
+        for ch in range(4):
+            square(ch)
+            if ch == 1:
+                nc.sync.dma_start(out=out_rows[:, :, 0:HALF], in_=y01[:])
+            if ch > 1:
+                nc.sync.dma_start(out=out_rows[:, :, 128 * ch : 128 * (ch + 1)], in_=ys[ch])
+        weave_v(nc, y_b[:, 0:512], ys[0])
+        weave_v(nc, y_b[:, 512:1024], ys[1])
+        weave_v(nc, y_b[:, 1024:1536], ys[2])
+        qy(0, 256)
+        nc.sync.dma_start(out=out_words[:, 0:HALF], in_=o_q[:, 0:HALF])
+        weave_v(nc, y_b[:, 1536:2048], ys[3])
+        qy(256, 128)
+        qy(384, 128)
+        nc.sync.dma_start(out=out_words[:, HALF:N], in_=o_q[:, HALF:N])
+        for q in range(4):
+            eng = nc.sync if q % 2 == 0 else nc.scalar
+            eng.dma_start(out=out_2[0, 4 * q : 4 * q + 4, :].bitcast(I32), in_=o_s[32 * q : 32 * q + 4, :].bitcast(I32))

@@ -1,6 +1,7 @@
 from contextlib import ExitStack
 
 import concourse.mybir as mybir
+from concourse.masks import make_identity
 
 K, T, S, N, H = 512, 2048, 512, 512, 512
 FLOPS = 4 * 2 * 512 * 512 * 512
@@ -60,17 +61,23 @@ def tile_picked_momdiff_square_po_kernel(tc, x_words, x_scales, wa, wb, gt, gi, 
             nc.sync.dma_start(out=xs[32 * q : 32 * q + 4, :].bitcast(I32), in_=x_scales[0, 4 * q : 4 * q + 4, :].bitcast(I32))
         raw = {}
         nc.sync.dma_start(out=xw[:], in_=x_words[0].rearrange("p n t -> p (n t)").bitcast(I32))
+        gsrc = tile("gsrc", [P, P], F32)
+        nc.vector.memset(gsrc[:], 0.0)
+        nc.sync.dma_start(out=gsrc[0:4, :].rearrange("t (q s) -> t q s", s=8), in_=gi.rearrange("(q t s) o -> t q (s o)", t=4, s=8))
+        nc.sync.dma_start(out=gsrc[4:8, :].rearrange("t (q s) -> t q s", s=8), in_=gt.rearrange("(q t s) o -> t q (s o)", t=4, s=8))
         for nm, w in (("b", wb), ("a", wa)):
             for h in range(2):
                 raw[nm, h] = tile("w%s_raw%d" % (nm, h), [P, 4, HALF], F32)
                 nc.sync.dma_start(out=raw[nm, h][:], in_=w.rearrange("(p j) n -> p j n", j=4)[:, :, h * HALF : (h + 1) * HALF])
-        gt_t = tile("gt_t", [P, 4], F32)
-        gi_t = tile("gi_t", [P, 4], F32)
-        nc.sync.dma_start(out=gi_t[:], in_=gi.rearrange("(p t) o -> p (t o)", t=4))
-        nc.sync.dma_start(out=gt_t[:], in_=gt.rearrange("(p t) o -> p (t o)", t=4))
+        ident = tile("ident", [P, P], F32)
+        make_identity(nc, ident[:])
+        gps = psum.tile([P, P], F32, name="bank7")
+        nc.tensor.transpose(gps[:], gsrc[:], ident[:])
+        gains = tile("gains", [P, 8], F32)
+        nc.scalar.copy(out=gains[:], in_=gps[:, 0:8])
         warm = tile("warm", [P, 8], F32)
         warm2 = tile("warm2", [P, 8], F32)
-        nc.gpsimd.memset(warm[:], 0.0)
+        nc.vector.memset(warm[:], 0.0)
         nc.scalar.activation(out=warm2[:], in_=warm[:], func=ACT.Square)
 
         def pick_scales(name, lst):
@@ -80,31 +87,32 @@ def tile_picked_momdiff_square_po_kernel(tc, x_words, x_scales, wa, wb, gt, gi, 
             return g, d
 
         def deal_scales(g, d):
-            nc.vector.tensor_copy(out=d[:].rearrange("p (t m) -> p t m", t=4), in_=g[:].rearrange("p (m t) -> p t m", t=4))
+            nc.vector.tensor_copy(out=d[:].bitcast(I32).rearrange("p (t q e) -> p t q e", t=4, e=2), in_=g[:].bitcast(I32).rearrange("p (q t e) -> p t q e", t=4, e=2))
 
-        def pick_words(name, lst):
-            g = tile(name + "_w", [P, S], U32)
-            nc.vector.tensor_copy(out=g[:].rearrange("p (t m) -> p m t", t=4), in_=xw[:].bitcast(U32).indirect(lst[:]))
+        def pick_words(name, lst, tag=None):
+            g = tile(name + "_w", [P, S], U32, tag)
+            nc.vector.tensor_copy(out=g[:].rearrange("p (t q s) -> p q t s", t=4, s=8), in_=xw[:].bitcast(U32).indirect(lst[:]))
             return g
 
         def mm(out, lq, ls, rq, rs, start=True, stop=True):
             nc.tensor.matmul_mx(out=out, lhsT=lq.bitcast(X4), lhsT_scale=ls, rhs=rq.bitcast(X4), rhs_scale=rs, start=start, stop=stop)
 
         g2, s2 = pick_scales("two", two_t)
+        g1, s1 = pick_scales("offs", offs_t)
         w2 = pick_words("two", two_t)
         deal_scales(g2, s2)
-        g1, s1 = pick_scales("offs", offs_t)
+        deal_scales(g1, s1)
 
-        wb_b = tile("wb_b", [P, 4 * N], BF16)
+        wb_b = [tile("wb_b%d" % h, [P, 4 * HALF], BF16) for h in range(2)]
         wb_q = tile("wb_q", [P, N], U32)
         wb_s = tile("wb_s", [P, N], U8)
-        for h in range(2):
-            weave_s(nc, wb_b[:, 4 * HALF * h : 4 * HALF * (h + 1)], raw["b", h][:])
         w1 = pick_words("offs", offs_t)
+        weave_s(nc, wb_b[0][:], raw["b", 0][:])
+        weave_s(nc, wb_b[1][:, 0:512], raw["b", 1][:, :, 0:128])
+        weave_v(nc, wb_b[1][:, 512:1024], raw["b", 1][:, :, 128:256])
         for h in range(2):
             c = slice(h * HALF, (h + 1) * HALF)
-            quant("wb", wb_b[:, 4 * HALF * h : 4 * HALF * (h + 1)], wb_q[:, c], wb_s[:, c])
-        deal_scales(g1, s1)
+            quant("wb", wb_b[h][:], wb_q[:, c], wb_s[:, c])
 
         banks = {}
         for t in range(4):
@@ -115,18 +123,18 @@ def tile_picked_momdiff_square_po_kernel(tc, x_words, x_scales, wa, wb, gt, gi, 
         wa_b = tile("wa_b", [P, 4 * H], BF16)
         wa_q = tile("wa_q", [P, H], U32)
         wa_s = tile("wa_s", [P, H], U8)
-        weave_s(nc, wa_b[:, 0 : 4 * HALF], raw["a", 0][:])
-        weave_v(nc, wa_b[:, 4 * HALF : 8 * HALF], raw["a", 1][:])
-        for h in range(2):
-            c = slice(h * HALF, (h + 1) * HALF)
-            quant("wa", wa_b[:, 4 * HALF * h : 4 * HALF * (h + 1)], wa_q[:, c], wa_s[:, c])
+        weave_s(nc, wa_b[:, 0:512], raw["a", 0][:, :, 0:128])
+        weave_v(nc, wa_b[:, 512:1024], raw["a", 0][:, :, 128:256])
+        quant("wa", wa_b[:, 0:1024], wa_q[:, 0:HALF], wa_s[:, 0:HALF])
+        weave_v(nc, wa_b[:, 1024:2048], raw["a", 1][:])
+        quant("wa", wa_b[:, 1024:2048], wa_q[:, HALF:H], wa_s[:, HALF:H])
 
         win = []
         z2f = tile("z2f", [P, 4, N], F32)
         for t in range(4):
             wt = tile("win%d" % t, [P, N], F32)
             win.append(wt)
-            nc.scalar.activation(out=wt[:], in_=banks["b", t][:], func=ACT.Copy, scale=gi_t[:, t : t + 1])
+            nc.scalar.activation(out=wt[:], in_=banks["b", t][:], func=ACT.Copy, scale=gains[:, t : t + 1])
             nc.sync.dma_start(out=z2f[:, t, :], in_=wt[:])
 
         for t in range(4):
@@ -135,8 +143,8 @@ def tile_picked_momdiff_square_po_kernel(tc, x_words, x_scales, wa, wb, gt, gi, 
             mm(banks["a", t][:], w1[:, c], s1[:, c], wa_q[:], wa_s[:])
 
         spans = [(0, 256), (256, 128), (384, 128)]
-        z3f = [tile("z3f%d" % i, [P, 4, w], F32) for i, (c0, w) in enumerate(spans[0:2])]
-        z3b = [tile("z3b%d" % i, [P, 4 * w], BF16) for i, (c0, w) in enumerate(spans)]
+        z3f = [tile("z3f0", [P, 4, HALF], F32, tag="wa_b"), tile("z3f1", [P, 4, 128], F32, tag="wa_raw1")]
+        z3b = {0: tile("z3b0", [P, 4 * HALF], BF16)}
         z3q = tile("z3q", [P, N], U32)
         z3s = tile("z3s", [P, N], U8)
         z2b = [tile("z2b%d" % h, [P, 4 * HALF], BF16) for h in range(2)]
@@ -158,7 +166,7 @@ def tile_picked_momdiff_square_po_kernel(tc, x_words, x_scales, wa, wb, gt, gi, 
         gather(0, range(4))
         zp = tile("zp", [P, 4, H], BF16)
         for t in range(4):
-            nc.scalar.activation(out=zp[:, t, :].rearrange("p (u m) -> p u m", u=4), in_=banks["a", t][:].rearrange("p (m u) -> p u m", u=4), func=ACT.Copy, scale=gt_t[:, t : t + 1])
+            nc.scalar.activation(out=zp[:, t, :].rearrange("p (u m) -> p u m", u=4), in_=banks["a", t][:].rearrange("p (m u) -> p u m", u=4), func=ACT.Copy, scale=gains[:, 4 + t : 5 + t])
         gather(1, range(4))
         z_b = [tile("z_b%d" % h, [P, 4 * HALF], BF16) for h in range(2)]
         z_q = tile("z_q", [P, H], U32)
@@ -170,57 +178,75 @@ def tile_picked_momdiff_square_po_kernel(tc, x_words, x_scales, wa, wb, gt, gi, 
         weave_s(nc, z2b[0][:], z2f[:, :, 0:HALF])
         for h in range(2):
             quant("z", z_b[h][:], z_q[:, h * HALF : (h + 1) * HALF], z_s[:, h * HALF : (h + 1) * HALF])
-        weave_s(nc, z3b[1][:], z3f[1][:], -1.0)
         q2(0)
         weave_s(nc, z2b[1][:], z2f[:, :, HALF:N])
-        z3f.append(tile("z3f2", [P, 4, 128], F32, tag="z_b1"))
+        z3b[1] = tile("z3b1", [P, 512], BF16, tag="zp")
+        weave_s(nc, z3b[1][:], z3f[1][:], -1.0)
+        z3f.append(tile("z3f2", [P, 4, 128], F32, tag="z2b0"))
 
         o_q = tile("o_q", [P, N], I32)
         o_s = tile("o_s", [P, N], U8)
         out_rows = out_0.rearrange("(p u) n -> p u n", u=4)
         out_words = out_1[0].rearrange("p n t -> p (n t)").bitcast(I32)
-        y01 = tile("y01", [P, 4, HALF], F32)
-        ys = [y01[:, :, 0:128], y01[:, :, 128:256], tile("y2", [P, 4, 128], F32)[:], tile("y3", [P, 4, 128], F32)[:]]
+        ys = [tile("y%d" % i, [P, 4, w], F32) for i, (c0, w) in enumerate(spans)]
         y_b = tile("y_b", [P, 4 * N], BF16)
-        acc = {}
 
-        def product(ch):
-            acc[ch] = psum.tile([P, 4, 128], F32, name="bank%d" % ch)
-            cols = slice(128 * ch, 128 * (ch + 1))
-            for u in range(4):
-                c = slice(128 * u, 128 * (u + 1))
-                mm(acc[ch][:, u, :], z_q[:, c], z_s[:, c], z2q[:, cols], z2s[:, cols], True, False)
-                mm(acc[ch][:, u, :], z_q[:, c], z_s[:, c], z3q[:, cols], z3s[:, cols], False, True)
+        def final_pass(acc, u, i, second):
+            c0, w = spans[i]
+            c = slice(128 * u, 128 * (u + 1))
+            rq, rs = (z3q, z3s) if second == (i > 0) else (z2q, z2s)
+            mm(acc, z_q[:, c], z_s[:, c], rq[:, c0 : c0 + w], rs[:, c0 : c0 + w], not second, second)
 
-        def square(ch):
-            nc.scalar.activation(out=ys[ch], in_=acc[ch][:], func=ACT.Square, scale=0.03125)
+        def paired_product(i, first_bank):
+            c0, w = spans[i]
+            acc = [psum.tile([P, 2, w], F32, name="bank%d" % (first_bank + e)) for e in range(2)]
+            for v in range(2):
+                for second in (False, True):
+                    for e in range(2):
+                        final_pass(acc[e][:, v, :], 2 * e + v, i, second)
+            return acc
 
-        def qy(c0, w):
+        def square(dst, src):
+            nc.scalar.activation(out=dst, in_=src, func=ACT.Square, scale=0.03125)
+
+        def store_y(i):
+            c0, w = spans[i]
+            nc.sync.dma_start(out=out_rows[:, :, c0 : c0 + w], in_=ys[i][:])
+
+        def weave_y(i):
+            c0, w = spans[i]
+            weave_v(nc, y_b[:, 4 * c0 : 4 * (c0 + w)], ys[i][:])
+
+        def qy(i):
+            c0, w = spans[i]
             quant("y", y_b[:, 4 * c0 : 4 * (c0 + w)], o_q[:, c0 : c0 + w], o_s[:, c0 : c0 + w])
 
-        product(0)
-        product(1)
+        acc0 = [psum.tile([P, HALF], F32, name="bank%d" % u) for u in range(4)]
+        for second in (False, True):
+            for u in range(4):
+                final_pass(acc0[u][:], u, 0, second)
         gather(2, range(4))
-        q3(1)
-        weave_v(nc, z3b[2][:], z3f[2][:], -1.0)
         q2(1)
+        q3(1)
+        z3b[2] = tile("z3b2", [P, 512], BF16, tag="zp")
+        weave_v(nc, z3b[2][:], z3f[2][:], -1.0)
         q3(2)
-        product(2)
-        product(3)
-        for ch in range(4):
-            square(ch)
-            if ch == 1:
-                nc.sync.dma_start(out=out_rows[:, :, 0:HALF], in_=y01[:])
-            if ch > 1:
-                nc.sync.dma_start(out=out_rows[:, :, 128 * ch : 128 * (ch + 1)], in_=ys[ch])
-        weave_v(nc, y_b[:, 0:512], ys[0])
-        weave_v(nc, y_b[:, 512:1024], ys[1])
-        weave_v(nc, y_b[:, 1024:1536], ys[2])
-        qy(0, 256)
+        acc1 = paired_product(1, 4)
+        acc2 = paired_product(2, 6)
+        for u in range(4):
+            square(ys[0][:, u, :], acc0[u][:])
+        store_y(0)
+        for i, acc in ((1, acc1), (2, acc2)):
+            for e in range(2):
+                square(ys[i][:, 2 * e : 2 * e + 2, :], acc[e][:])
+            store_y(i)
+        weave_y(0)
+        weave_y(1)
+        qy(0)
         nc.sync.dma_start(out=out_words[:, 0:HALF], in_=o_q[:, 0:HALF])
-        weave_v(nc, y_b[:, 1536:2048], ys[3])
-        qy(256, 128)
-        qy(384, 128)
+        weave_y(2)
+        qy(1)
+        qy(2)
         nc.sync.dma_start(out=out_words[:, HALF:N], in_=o_q[:, HALF:N])
         for q in range(4):
             eng = nc.sync if q % 2 == 0 else nc.scalar

@@ -65,7 +65,9 @@ def tile_picked_momdiff_square_po_kernel(tc, x_words, x_scales, wa, wb, gt, gi, 
         nc.vector.memset(gsrc[:], 0.0)
         nc.sync.dma_start(out=gsrc[0:4, :].rearrange("t (q s) -> t q s", s=8), in_=gi.rearrange("(q t s) o -> t q (s o)", t=4, s=8))
         nc.sync.dma_start(out=gsrc[4:8, :].rearrange("t (q s) -> t q s", s=8), in_=gt.rearrange("(q t s) o -> t q (s o)", t=4, s=8))
-        for nm, w in (("b", wb), ("a", wa)):
+        wb_raw = tile("wb_raw", [P, 4, N], F32)
+        nc.sync.dma_start(out=wb_raw[:], in_=wb.rearrange("(p j) n -> p j n", j=4))
+        for nm, w in (("a", wa),):
             for h in range(2):
                 raw[nm, h] = tile("w%s_raw%d" % (nm, h), [P, 4, HALF], F32)
                 nc.sync.dma_start(out=raw[nm, h][:], in_=w.rearrange("(p j) n -> p j n", j=4)[:, :, h * HALF : (h + 1) * HALF])
@@ -103,16 +105,16 @@ def tile_picked_momdiff_square_po_kernel(tc, x_words, x_scales, wa, wb, gt, gi, 
         deal_scales(g2, s2)
         deal_scales(g1, s1)
 
-        wb_b = [tile("wb_b%d" % h, [P, 4 * HALF], BF16) for h in range(2)]
+        wb_b = tile("wb_b", [P, 4 * N], BF16)
         wb_q = tile("wb_q", [P, N], U32)
         wb_s = tile("wb_s", [P, N], U8)
         w1 = pick_words("offs", offs_t)
-        weave_s(nc, wb_b[0][:], raw["b", 0][:])
-        weave_s(nc, wb_b[1][:, 0:512], raw["b", 1][:, :, 0:128])
-        weave_v(nc, wb_b[1][:, 512:1024], raw["b", 1][:, :, 128:256])
+        weave_s(nc, wb_b[:, 1280:2048], wb_raw[:, :, 320:512])
+        weave_v(nc, wb_b[:, 0:1024], wb_raw[:, :, 0:256])
+        weave_v(nc, wb_b[:, 1024:1280], wb_raw[:, :, 256:320])
         for h in range(2):
             c = slice(h * HALF, (h + 1) * HALF)
-            quant("wb", wb_b[h][:], wb_q[:, c], wb_s[:, c])
+            quant("wb", wb_b[:, 1024 * h : 1024 * (h + 1)], wb_q[:, c], wb_s[:, c])
 
         banks = {}
         for t in range(4):
@@ -126,8 +128,10 @@ def tile_picked_momdiff_square_po_kernel(tc, x_words, x_scales, wa, wb, gt, gi, 
         weave_s(nc, wa_b[:, 0:512], raw["a", 0][:, :, 0:128])
         weave_v(nc, wa_b[:, 512:1024], raw["a", 0][:, :, 128:256])
         quant("wa", wa_b[:, 0:1024], wa_q[:, 0:HALF], wa_s[:, 0:HALF])
-        weave_v(nc, wa_b[:, 1024:2048], raw["a", 1][:])
-        quant("wa", wa_b[:, 1024:2048], wa_q[:, HALF:H], wa_s[:, HALF:H])
+        weave_v(nc, wa_b[:, 1024:1536], raw["a", 1][:, :, 0:128])
+        weave_v(nc, wa_b[:, 1536:2048], raw["a", 1][:, :, 128:256])
+        quant("wa", wa_b[:, 1024:1536], wa_q[:, 256:384], wa_s[:, 256:384])
+        quant("wa", wa_b[:, 1536:2048], wa_q[:, 384:512], wa_s[:, 384:512])
 
         win = []
         z2f = tile("z2f", [P, 4, N], F32)
@@ -176,7 +180,7 @@ def tile_picked_momdiff_square_po_kernel(tc, x_words, x_scales, wa, wb, gt, gi, 
         weave_v(nc, z_b[0][:], zp[:, :, 0:HALF])
         q3(0)
         weave_s(nc, z2b[0][:], z2f[:, :, 0:HALF])
-        for h in range(2):
+        for h in (1, 0):
             quant("z", z_b[h][:], z_q[:, h * HALF : (h + 1) * HALF], z_s[:, h * HALF : (h + 1) * HALF])
         q2(0)
         weave_s(nc, z2b[1][:], z2f[:, :, HALF:N])
@@ -223,7 +227,7 @@ def tile_picked_momdiff_square_po_kernel(tc, x_words, x_scales, wa, wb, gt, gi, 
 
         acc0 = [psum.tile([P, HALF], F32, name="bank%d" % u) for u in range(4)]
         for second in (False, True):
-            for u in range(4):
+            for u in (2, 3, 0, 1):
                 final_pass(acc0[u][:], u, 0, second)
         gather(2, range(4))
         q2(1)
@@ -233,7 +237,7 @@ def tile_picked_momdiff_square_po_kernel(tc, x_words, x_scales, wa, wb, gt, gi, 
         q3(2)
         acc1 = paired_product(1, 4)
         acc2 = paired_product(2, 6)
-        for u in range(4):
+        for u in (2, 3, 0, 1):
             square(ys[0][:, u, :], acc0[u][:])
         store_y(0)
         for i, acc in ((1, acc1), (2, acc2)):

from contextlib import ExitStack

import concourse.mybir as mybir
from concourse.masks import make_identity

K, T, S, N, H = 512, 2048, 512, 512, 512
FLOPS = 4 * 2 * 512 * 512 * 512

F32 = mybir.dt.float32
BF16 = mybir.dt.bfloat16
I32 = mybir.dt.int32
U32 = mybir.dt.uint32
U16 = mybir.dt.uint16
U8 = mybir.dt.uint8
X4 = mybir.dt.float8_e4m3fn_x4
ACT = mybir.ActivationFunctionType
ALU = mybir.AluOpType
P = 128
HALF = 256


def weave_views(dst, src):
    return dst.rearrange("p (c i t) -> p c t i", i=4, t=4), src.rearrange("p t (c i) -> p c t i", i=4)


def weave_v(nc, dst, src, scale=None):
    d, s = weave_views(dst, src)
    if scale is None:
        nc.vector.tensor_copy(out=d, in_=s)
    else:
        nc.vector.tensor_scalar(out=d, in0=s, scalar1=scale, scalar2=None, op0=ALU.mult)


def weave_s(nc, dst, src, scale=1.0):
    d, s = weave_views(dst, src)
    nc.scalar.activation(out=d, in_=s, func=ACT.Copy, scale=scale)


def tile_picked_momdiff_square_po_kernel(tc, x_words, x_scales, wa, wb, gt, gi, offs, two, fl, out_0, out_1, out_2):
    nc = tc.nc
    with ExitStack() as ctx:
        keep = ctx.enter_context(tc.tile_pool(name="keep", bufs=1))
        psum = ctx.enter_context(tc.psum_pool(name="psum", bufs=1))

        def tile(name, shape, dtype, tag=None):
            return keep.tile(shape, dtype, name=name, tag=tag or name, align_bytes=64)

        def quant(name, src, codes, scales):
            nc.vector.quantize_mx(out=codes.bitcast(X4), scales=scales, in_=src)

        two_t = keep.tile([P, 32], U16, name="two_t")
        offs_t = keep.tile([P, 32], U16, name="offs_t")
        fl_t = keep.tile([P, 32], U16, name="fl_t")
        xw = tile("xw", [P, T], I32)
        xs = tile("xs", [P, T], U8)
        nc.vector.memset(xs[:].bitcast(I32), 0)
        nc.sync.dma_start(two_t[:], two)
        nc.sync.dma_start(offs_t[:], offs)
        nc.sync.dma_start(fl_t[:], fl)
        for q in range(4):
            nc.sync.dma_start(out=xs[32 * q : 32 * q + 4, :].bitcast(I32), in_=x_scales[0, 4 * q : 4 * q + 4, :].bitcast(I32))
        raw = {}
        nc.sync.dma_start(out=xw[:], in_=x_words[0].rearrange("p n t -> p (n t)").bitcast(I32))
        gsrc = tile("gsrc", [P, P], F32)
        nc.vector.memset(gsrc[:], 0.0)
        nc.sync.dma_start(out=gsrc[0:4, :].rearrange("t (q s) -> t q s", s=8), in_=gi.rearrange("(q t s) o -> t q (s o)", t=4, s=8))
        nc.sync.dma_start(out=gsrc[4:8, :].rearrange("t (q s) -> t q s", s=8), in_=gt.rearrange("(q t s) o -> t q (s o)", t=4, s=8))
        wb_raw = tile("wb_raw", [P, 4, N], F32)
        nc.sync.dma_start(out=wb_raw[:], in_=wb.rearrange("(p j) n -> p j n", j=4))
        for nm, w in (("a", wa),):
            for h in range(2):
                raw[nm, h] = tile("w%s_raw%d" % (nm, h), [P, 4, HALF], F32)
                nc.sync.dma_start(out=raw[nm, h][:], in_=w.rearrange("(p j) n -> p j n", j=4)[:, :, h * HALF : (h + 1) * HALF])
        ident = tile("ident", [P, P], F32)
        make_identity(nc, ident[:])
        gps = psum.tile([P, P], F32, name="bank7")
        nc.tensor.transpose(gps[:], gsrc[:], ident[:])
        gains = tile("gains", [P, 8], F32)
        nc.scalar.copy(out=gains[:], in_=gps[:, 0:8])
        warm = tile("warm", [P, 8], F32)
        warm2 = tile("warm2", [P, 8], F32)
        nc.vector.memset(warm[:], 0.0)
        nc.scalar.activation(out=warm2[:], in_=warm[:], func=ACT.Square)

        def pick_scales(name, lst):
            g = tile(name + "_g", [P, S], U8)
            nc.vector.tensor_copy(out=g[:], in_=xs[:].indirect(lst[:]))
            d = tile(name + "_d", [P, S], U8)
            return g, d

        def deal_scales(g, d):
            nc.vector.tensor_copy(out=d[:].bitcast(I32).rearrange("p (t q e) -> p t q e", t=4, e=2), in_=g[:].bitcast(I32).rearrange("p (q t e) -> p t q e", t=4, e=2))

        def pick_words(name, lst, tag=None):
            g = tile(name + "_w", [P, S], U32, tag)
            nc.vector.tensor_copy(out=g[:].rearrange("p (t q s) -> p q t s", t=4, s=8), in_=xw[:].bitcast(U32).indirect(lst[:]))
            return g

        def mm(out, lq, ls, rq, rs, start=True, stop=True):
            nc.tensor.matmul_mx(out=out, lhsT=lq.bitcast(X4), lhsT_scale=ls, rhs=rq.bitcast(X4), rhs_scale=rs, start=start, stop=stop)

        g2, s2 = pick_scales("two", two_t)
        g1, s1 = pick_scales("offs", offs_t)
        w2 = pick_words("two", two_t)
        deal_scales(g2, s2)
        deal_scales(g1, s1)

        wb_b = tile("wb_b", [P, 4 * N], BF16)
        wb_q = tile("wb_q", [P, N], U32)
        wb_s = tile("wb_s", [P, N], U8)
        w1 = pick_words("offs", offs_t)
        weave_s(nc, wb_b[:, 1280:2048], wb_raw[:, :, 320:512])
        weave_v(nc, wb_b[:, 0:1024], wb_raw[:, :, 0:256])
        weave_v(nc, wb_b[:, 1024:1280], wb_raw[:, :, 256:320])
        for h in range(2):
            c = slice(h * HALF, (h + 1) * HALF)
            quant("wb", wb_b[:, 1024 * h : 1024 * (h + 1)], wb_q[:, c], wb_s[:, c])

        banks = {}
        for t in range(4):
            banks["b", t] = psum.tile([P, N], F32, name="bank%d" % t)
            c = slice(128 * t, 128 * (t + 1))
            mm(banks["b", t][:], w2[:, c], s2[:, c], wb_q[:], wb_s[:])

        wa_b = tile("wa_b", [P, 4 * H], BF16)
        wa_q = tile("wa_q", [P, H], U32)
        wa_s = tile("wa_s", [P, H], U8)
        weave_s(nc, wa_b[:, 0:512], raw["a", 0][:, :, 0:128])
        weave_v(nc, wa_b[:, 512:1024], raw["a", 0][:, :, 128:256])
        quant("wa", wa_b[:, 0:1024], wa_q[:, 0:HALF], wa_s[:, 0:HALF])
        weave_v(nc, wa_b[:, 1024:1536], raw["a", 1][:, :, 0:128])
        weave_v(nc, wa_b[:, 1536:2048], raw["a", 1][:, :, 128:256])
        quant("wa", wa_b[:, 1024:1536], wa_q[:, 256:384], wa_s[:, 256:384])
        quant("wa", wa_b[:, 1536:2048], wa_q[:, 384:512], wa_s[:, 384:512])

        win = []
        z2f = tile("z2f", [P, 4, N], F32)
        for t in range(4):
            wt = tile("win%d" % t, [P, N], F32)
            win.append(wt)
            nc.scalar.activation(out=wt[:], in_=banks["b", t][:], func=ACT.Copy, scale=gains[:, t : t + 1])
            nc.sync.dma_start(out=z2f[:, t, :], in_=wt[:])

        for t in range(4):
            banks["a", t] = psum.tile([P, H], F32, name="bank%d" % (4 + t))
            c = slice(128 * t, 128 * (t + 1))
            mm(banks["a", t][:], w1[:, c], s1[:, c], wa_q[:], wa_s[:])

        spans = [(0, 256), (256, 128), (384, 128)]
        z3f = [tile("z3f0", [P, 4, HALF], F32, tag="wa_b"), tile("z3f1", [P, 4, 128], F32, tag="wa_raw1")]
        z3b = {0: tile("z3b0", [P, 4 * HALF], BF16)}
        z3q = tile("z3q", [P, N], U32)
        z3s = tile("z3s", [P, N], U8)
        z2b = [tile("z2b%d" % h, [P, 4 * HALF], BF16) for h in range(2)]
        z2q = tile("z2q", [P, N], U32)
        z2s = tile("z2s", [P, N], U8)

        def gather(i, ts):
            c0, w = spans[i]
            for t in ts:
                nc.vector.tensor_copy(out=z3f[i][:, t, :], in_=win[t][:].indirect(fl_t[:, c0 // 16 : (c0 + w) // 16]))

        def q3(i):
            c0, w = spans[i]
            quant("z3", z3b[i][:], z3q[:, c0 : c0 + w], z3s[:, c0 : c0 + w])

        def q2(h):
            quant("z2", z2b[h][:], z2q[:, h * HALF : (h + 1) * HALF], z2s[:, h * HALF : (h + 1) * HALF])

        gather(0, range(4))
        zp = tile("zp", [P, 4, H], BF16)
        for t in range(4):
            nc.scalar.activation(out=zp[:, t, :].rearrange("p (u m) -> p u m", u=4), in_=banks["a", t][:].rearrange("p (m u) -> p u m", u=4), func=ACT.Copy, scale=gains[:, 4 + t : 5 + t])
        gather(1, range(4))
        z_b = [tile("z_b%d" % h, [P, 4 * HALF], BF16) for h in range(2)]
        z_q = tile("z_q", [P, H], U32)
        z_s = tile("z_s", [P, H], U8)
        weave_s(nc, z_b[1][:], zp[:, :, HALF:H])
        weave_v(nc, z3b[0][:], z3f[0][:], -1.0)
        weave_v(nc, z_b[0][:], zp[:, :, 0:HALF])
        q3(0)
        weave_s(nc, z2b[0][:], z2f[:, :, 0:HALF])
        for h in (1, 0):
            quant("z", z_b[h][:], z_q[:, h * HALF : (h + 1) * HALF], z_s[:, h * HALF : (h + 1) * HALF])
        q2(0)
        weave_s(nc, z2b[1][:], z2f[:, :, HALF:N])
        z3b[1] = tile("z3b1", [P, 512], BF16, tag="zp")
        weave_s(nc, z3b[1][:], z3f[1][:], -1.0)
        z3f.append(tile("z3f2", [P, 4, 128], F32, tag="z2b0"))

        o_q = tile("o_q", [P, N], I32)
        o_s = tile("o_s", [P, N], U8)
        out_rows = out_0.rearrange("(p u) n -> p u n", u=4)
        out_words = out_1[0].rearrange("p n t -> p (n t)").bitcast(I32)
        ys = [tile("y%d" % i, [P, 4, w], F32) for i, (c0, w) in enumerate(spans)]
        y_b = tile("y_b", [P, 4 * N], BF16)

        def final_pass(acc, u, i, second):
            c0, w = spans[i]
            c = slice(128 * u, 128 * (u + 1))
            rq, rs = (z3q, z3s) if second == (i > 0) else (z2q, z2s)
            mm(acc, z_q[:, c], z_s[:, c], rq[:, c0 : c0 + w], rs[:, c0 : c0 + w], not second, second)

        def paired_product(i, first_bank):
            c0, w = spans[i]
            acc = [psum.tile([P, 2, w], F32, name="bank%d" % (first_bank + e)) for e in range(2)]
            for v in range(2):
                for second in (False, True):
                    for e in range(2):
                        final_pass(acc[e][:, v, :], 2 * e + v, i, second)
            return acc

        def square(dst, src):
            nc.scalar.activation(out=dst, in_=src, func=ACT.Square, scale=0.03125)

        def store_y(i):
            c0, w = spans[i]
            nc.sync.dma_start(out=out_rows[:, :, c0 : c0 + w], in_=ys[i][:])

        def weave_y(i):
            c0, w = spans[i]
            weave_v(nc, y_b[:, 4 * c0 : 4 * (c0 + w)], ys[i][:])

        def qy(i):
            c0, w = spans[i]
            quant("y", y_b[:, 4 * c0 : 4 * (c0 + w)], o_q[:, c0 : c0 + w], o_s[:, c0 : c0 + w])

        acc0 = [psum.tile([P, HALF], F32, name="bank%d" % u) for u in range(4)]
        for second in (False, True):
            for u in (2, 3, 0, 1):
                final_pass(acc0[u][:], u, 0, second)
        gather(2, range(4))
        q2(1)
        q3(1)
        z3b[2] = tile("z3b2", [P, 512], BF16, tag="zp")
        weave_v(nc, z3b[2][:], z3f[2][:], -1.0)
        q3(2)
        acc1 = paired_product(1, 4)
        acc2 = paired_product(2, 6)
        for u in (2, 3, 0, 1):
            square(ys[0][:, u, :], acc0[u][:])
        store_y(0)
        for i, acc in ((1, acc1), (2, acc2)):
            for e in range(2):
                square(ys[i][:, 2 * e : 2 * e + 2, :], acc[e][:])
            store_y(i)
        weave_y(0)
        weave_y(1)
        qy(0)
        nc.sync.dma_start(out=out_words[:, 0:HALF], in_=o_q[:, 0:HALF])
        weave_y(2)
        qy(1)
        qy(2)
        nc.sync.dma_start(out=out_words[:, HALF:N], in_=o_q[:, HALF:N])
        for q in range(4):
            eng = nc.sync if q % 2 == 0 else nc.scalar
            eng.dma_start(out=out_2[0, 4 * q : 4 * q + 4, :].bitcast(I32), in_=o_s[32 * q : 32 * q + 4, :].bitcast(I32))
